import numpy as np
import ml_dtypes


def mxq(x, axis, fmt="e4m3"):
    dtype, down = {"e4m3": (ml_dtypes.float8_e4m3fn, 7), "e5m2": (ml_dtypes.float8_e5m2, 14)}[fmt]
    v = np.moveaxis(np.asarray(x, np.float32).astype(ml_dtypes.bfloat16).astype(np.float64), axis, -1)
    blocks = v.reshape(v.shape[:-1] + (-1, 32))
    amax = np.abs(blocks).max(-1, keepdims=True)
    byte = np.maximum(np.where(amax > 0, np.frexp(amax)[1] - 1 + 127, 0) - down, 1)
    scale = np.exp2(byte - 127.0)
    codes = (blocks / scale).astype(np.float32).astype(dtype).astype(np.float64)
    return np.moveaxis((codes * scale).reshape(v.shape), -1, axis)


WIDE = False


def mx_kscale(k):
    if not WIDE:
        return np.ones(k)
    levels = np.array([10, -10, 5, -5, 0])
    if k % 512:
        return np.exp2(np.random.permutation(np.resize(levels, k // 32))).repeat(32)
    a = np.empty((k // 512, 16))
    for p in range(k // 512):
        a[p, :8] = np.random.permutation(np.resize(levels, 8))
        for g in range(8):
            far = levels[np.abs(levels - a[p, g]) >= 10]
            a[p, g + 8] = far[np.random.randint(len(far))]
    return np.exp2(a.ravel()).repeat(32)


def f64(x):
    return np.asarray(x).astype(np.float64)


def striped(idx):
    return np.tile(idx.reshape(-1, 16).T, (8, 1)).astype(np.uint16)


def unstriped(offs):
    return offs[:16].T.reshape(-1).astype(np.int64)


E2M1 = np.array([0.0, 0.5, 1.0, 1.5, 2.0, 3.0, 4.0, 6.0, -0.0, -0.5, -1.0, -1.5, -2.0, -3.0, -4.0, -6.0])


def pack_weight(w, fmt):
    k, n = w.shape
    w = f64(np.asarray(w, np.float32).astype(ml_dtypes.bfloat16)).reshape(k // 32, 32, n)
    amax = np.abs(w).max(1)
    if fmt == "e4m3":
        byte = np.frexp(amax)[1] - 1 + 127 - 7
    else:
        mant, ex = np.frexp(amax / 6.0)
        byte = np.where(mant > 0.5, ex, ex - 1) + 127
    byte = np.clip(np.where(amax > 0, byte, 1), 1, 254)
    scaled = (w * np.exp2(127.0 - byte)[:, None, :]).reshape(k, n).astype(np.float32)
    by_word = np.ascontiguousarray(scaled.reshape(k // 512, 128, 4, n).transpose(0, 1, 3, 2))
    if fmt == "e4m3":
        words = by_word.astype(ml_dtypes.float8_e4m3fn).view(np.uint8)
    else:
        c = by_word.astype(ml_dtypes.float4_e2m1fn).view(np.uint8) & 0xF
        words = (c[..., 0::2] | (c[..., 1::2] << 4)).reshape(k // 512, 128, 2 * n)
    return np.ascontiguousarray(words), np.ascontiguousarray(byte.astype(np.uint8).reshape(k // 512, 16, n))


def unpack_weight(words, scales, fmt):
    g, _, n = scales.shape
    words = np.ascontiguousarray(words).reshape(g, 128, n, -1)
    if fmt == "e4m3":
        vals = words.view(ml_dtypes.float8_e4m3fn).astype(np.float64)
    else:
        nib = np.empty((g, 128, n, 4), np.uint8)
        nib[..., 0::2] = words & 0xF
        nib[..., 1::2] = words >> 4
        vals = E2M1[nib]
    vals = vals * np.repeat(np.exp2(scales.astype(np.float64) - 127.0), 8, axis=1)[..., None]
    return vals.transpose(0, 1, 3, 2).reshape(g * 512, n)


def gelu(v):
    return 0.5 * v * (1.0 + np.tanh(np.sqrt(2.0 / np.pi) * (v + 0.044715 * v**3)))


K, K2, H, N, T, TB, S, P = 1024, 512, 1024, 512, 4096, 2048, 1024, 512

def setup_inputs():
    n = np.random.standard_normal
    s, s2, u = mx_kscale(K)[:, None], mx_kscale(K2)[:, None], mx_kscale(H)[:, None]
    d = {}
    d["tab_words"], d["tab_scales"] = pack_weight(n((K, T)) * s, "e4m3")
    d["offs"] = striped(np.random.permutation(T)[:S])
    d["tab2_words"], d["tab2_scales"] = pack_weight(n((K2, TB)) * s2, "e4m3")
    d["offs2"] = striped(np.random.permutation(TB)[:P])
    d["pos1"] = striped(np.random.permutation(S)[:P])
    reach = 2.0 * np.exp(0.7 * n(H))
    d["w1_words"], d["w1_scales"] = pack_weight(n((H, K)).T * reach * (u * u).T / s / K**0.5, "e2m1")
    d["base"] = (np.exp(0.5 * n(H)) * u[:, 0]**2).astype(np.float32)
    d["w2"] = (2.0 * n((K2, H)) * u.T / s2 / K2**0.5).astype(np.float32)
    d["w3"] = (1.8 * n((K2, H)) / s2 / K2**0.5).astype(np.float32)
    d["wgs"] = np.exp(0.3 * n((128, P))).astype(np.float32)
    d["w4"] = (n((H, N)) / u / H**0.5).astype(np.float32)
    d["w5_words"], d["w5_scales"] = pack_weight(n((H, N)) / u / H**0.5, "e4m3")
    return d

def reference(tab_words, tab_scales, offs, tab2_words, tab2_scales, offs2, pos1, w1_words, w1_scales, base, w2, w3, wgs, w4, w5_words, w5_scales):
    v = unpack_weight(tab_words, tab_scales, "e4m3")[:, unstriped(offs)]
    v2 = unpack_weight(tab2_words, tab2_scales, "e4m3")[:, unstriped(offs2)]
    intake = unpack_weight(w1_words, w1_scales, "e2m1").T @ v
    a = np.sqrt(f64(base)[:, None] + np.abs(intake))
    left = mxq(f64(w2), 0, "e4m3").T @ v2
    kind = mxq(f64(w3), 0, "e4m3").T @ v2
    b = left * np.tanh(kind)
    placed = np.zeros((H, S))
    placed[:, unstriped(pos1)] = np.tile(f64(wgs), (H // 128, 1)) * b
    z = mxq(a - placed, 0, "e4m3")
    y1 = mxq(f64(w4), 0, "e4m3").T @ z
    y2 = unpack_weight(w5_words, w5_scales, "e4m3").T @ z
    return np.minimum(y1, y2)

@@ -1,0 +1,316 @@
+from contextlib import ExitStack
+
+import concourse.mybir as mybir
+from concourse.masks import make_identity
+
+K, K2, H, N, T, TB, S, P = 1024, 512, 1024, 512, 4096, 2048, 1024, 512
+FLOPS = 2 * K * H * S + 2 * 2 * K2 * H * P + 2 * 2 * H * N * S
+
+F32 = mybir.dt.float32
+BF16 = mybir.dt.bfloat16
+I32 = mybir.dt.int32
+U32 = mybir.dt.uint32
+U16 = mybir.dt.uint16
+U8 = mybir.dt.uint8
+FP8X4 = mybir.dt.float8_e4m3fn_x4
+FP4X4 = mybir.dt.float4_e2m1fn_x4
+ACT = mybir.ActivationFunctionType
+ALU = mybir.AluOpType
+
+PARTS = 128
+HALF = 512
+SLICES = H // PARTS
+PAGES = 3
+
+
+def tile_list_ration_adequacy_scores_kernel(
+    tc, tab_words, tab_scales, offs, tab2_words, tab2_scales, offs2, pos1, w1_words, w1_scales,
+    base, w2, w3, wgs, w4, w5_words, w5_scales, out,
+):
+    nc = tc.nc
+    with ExitStack() as ctx:
+        keep = ctx.enter_context(tc.tile_pool(name="keep", bufs=1))
+        psum = ctx.enter_context(tc.psum_pool(name="psum", bufs=1))
+
+        def sb(name, shape, dtype, tag=None):
+            return keep.tile(shape, dtype, name=name, tag=tag or name, align_bytes=64)
+
+        def bank(index, name):
+            return psum.tile([PARTS, HALF], F32, name=name, tag="bank%d" % index)
+
+        def load_scale_rows(queue, plane, scales):
+            for q in range(4):
+                queue.dma_start(
+                    out=plane[32 * q : 32 * q + 4, :, :].bitcast(I32),
+                    in_=scales[:, 4 * q : 4 * q + 4, :].rearrange("a r n -> r a n").bitcast(I32),
+                )
+
+        def load_rows(name, w, row0, col0, cols, tag=None):
+            raw = sb(name, [PARTS, 4, cols], F32, tag)
+            nc.sync.dma_start(
+                out=raw[:], in_=w[row0 : row0 + 512, col0 : col0 + cols].rearrange("(p t) c -> p t c", t=4)
+            )
+            return raw
+
+        def weave(copy, name, raw, col0, cols, tag=None):
+            woven = sb(name, [PARTS, cols, 4], BF16, tag)
+            copy(
+                woven[:].rearrange("p (c i) t -> p c t i", i=4),
+                raw[:, :, col0 : col0 + cols].rearrange("p t (c i) -> p c t i", i=4),
+            )
+            return woven
+
+        def quantize(name, woven, cols, tag=None, plane_tag=None):
+            codes = sb(name + "_codes", [PARTS, cols], U32, tag)
+            plane = sb(name + "_plane", [PARTS, cols], U8, plane_tag)
+            nc.vector.quantize_mx(
+                out=codes[:].bitcast(FP8X4), scales=plane[:], in_=woven.rearrange("p c t -> p (c t)")
+            )
+            return codes, plane
+
+        def mx(acc, lhs, lhs_plane, rhs, rhs_plane, start, stop):
+            nc.tensor.matmul_mx(
+                out=acc, lhsT=lhs, lhsT_scale=lhs_plane, rhs=rhs, rhs_scale=rhs_plane, start=start, stop=stop
+            )
+
+        tab2_plane = sb("tab2_plane", [PARTS, TB], U8)
+        warm = sb("warm", [PARTS, 1], F32)
+        nc.vector.memset(warm[:], 0.0)
+        warm_out = sb("warm_out", [PARTS, 2], F32)
+        nc.scalar.activation(warm_out[:, 0:1], warm[:], ACT.Tanh)
+        tab_plane = sb("tab_plane", [PARTS, T], U8)
+        nc.vector.memset(tab_plane[:].bitcast(I32), 0)
+        moved_plane = sb("moved_plane", [PARTS, S], U8)
+        pages = [sb("page%d" % i, [PARTS, S], F32) for i in range(PAGES)]
+        for words in [pages[0][:], moved_plane[:].bitcast(I32), pages[1][:], pages[2][:]]:
+            last = words.shape[1] - 1
+            nc.vector.memset(words[:, 0:last], 0)
+            nc.vector.memset(words[:, last : last + 1], 0)
+        for q in range(4):
+            nc.gpsimd.dma_start(
+                out=tab_plane[32 * q : 32 * q + 8, :].bitcast(I32),
+                in_=tab_scales[:, 4 * q : 4 * q + 4, :].bitcast(I32),
+            )
+
+        offs2_t = sb("offs2_t", [PARTS, P // 16], U16)
+        nc.sync.dma_start(offs2_t[:], offs2)
+        for q in range(4):
+            nc.sync.dma_start(
+                out=tab2_plane[32 * q : 32 * q + 32, :].bitcast(I32),
+                in_=tab2_scales[0, 4 * q : 4 * q + 4, :].bitcast(I32).unsqueeze(0).to_broadcast([8, 4, TB // 4]),
+            )
+        tab2_t = sb("tab2_t", [PARTS, TB], U32)
+        nc.sync.dma_start(out=tab2_t[:].bitcast(I32), in_=tab2_words[0].rearrange("p t i -> p (t i)").bitcast(I32))
+        w3_raw = [load_rows("w3_raw0", w3, 0, 0, 128)]
+        w2_raw = [load_rows("w2_raw0", w2, 0, 0, 256)]
+        offs_t = sb("offs_t", [PARTS, S // 16], U16)
+        nc.sync.dma_start(offs_t[:], offs)
+        wgs_t = sb("wgs_t", [PARTS, P], F32)
+        nc.sync.dma_start(out=wgs_t[:], in_=wgs)
+        pos_t = sb("pos_t", [PARTS, P // 16], U16)
+        nc.sync.dma_start(pos_t[:], pos1)
+
+        def w2_piece(c):
+            if c < 2:
+                return w2_raw[0], 128 * c
+            if c < 4:
+                return w2_raw[1], 128 * (c - 2)
+            return w2_raw[2], 128 * (c - 4)
+
+        v2_plane = sb("v2_plane", [PARTS, P], U8)
+        nc.vector.tensor_copy(v2_plane[:], tab2_plane[:].indirect(offs2_t[:]))
+        v2 = sb("v2", [PARTS, P], U32)
+        nc.vector.tensor_copy(v2[:], tab2_t[:].indirect(offs2_t[:]))
+
+        w3_raw.append(load_rows("w3_raw1", w3, 0, 128, 384, "tab2_plane"))
+        w3_raw.append(load_rows("w3_raw2", w3, 0, 512, 512, "tab2_t"))
+        neg_tanh = {}
+
+        w3_q = {}
+
+        def w3_part(first, count, raw, col0, woven):
+            nc.scalar.copy(
+                woven.rearrange("p (c i) t -> p c t i", i=4),
+                raw[:, :, col0 : col0 + 128 * count].rearrange("p t (c i) -> p c t i", i=4),
+            )
+            codes, plane = quantize("w3_%d" % first, woven, 128 * count, "w3_codes%d" % first if first else "picked", None if first else "tab_t0")
+            for i in range(count):
+                w3_q[first + i] = (codes[:, 128 * i : 128 * i + 128], plane[:, 128 * i : 128 * i + 128])
+
+        def kind_slice(c):
+            codes, plane = w3_q[c]
+            acc = bank((6, 7, 6, 7, 0, 1, 1, 0)[c], "kind%d" % c)
+            mx(acc[:], codes.bitcast(FP8X4), plane, v2[:].bitcast(FP8X4), v2_plane[:], True, True)
+            neg_tanh[c] = sb("neg_tanh%d" % c, [PARTS, P], F32)
+            nc.scalar.activation(neg_tanh[c][:], acc[:], ACT.Tanh, scale=-1.0)
+
+        def left_slice(c, index):
+            raw, col0 = w2_piece(c)
+            copy = nc.scalar.copy if c == 0 else nc.vector.tensor_copy
+            codes, plane = quantize("w2_%d" % c, weave(copy, "w2_woven%d" % c, raw, col0, 128, ("v_plane", "tab_plane", "tab_t1")[min(c, 2)])[:], 128, "w2_codes%d" % (c % 2) if c else "w1_t", None if c else "tab_t1")
+            acc = bank(index, "left%d" % c)
+            mx(acc[:], codes[:].bitcast(FP8X4), plane[:], v2[:].bitcast(FP8X4), v2_plane[:], True, True)
+            return acc
+
+        def place_slice(c, acc):
+            neg_b = sb("neg_b%d" % c, [PARTS, P], F32, "neg_b%d" % (c % 2) if c else "tab_plane")
+            nc.vector.tensor_tensor(neg_b[:], acc[:], neg_tanh[c][:], ALU.mult)
+            nc.vector.tensor_tensor(pages[c % PAGES][:].indirect(pos_t[:]), neg_b[:], wgs_t[:], ALU.mult)
+
+        w3_part(0, 1, w3_raw[0], 0, sb("w3_woven0", [PARTS, 128, 4], BF16)[:])
+        kind_slice(0)
+        left0 = left_slice(0, 2)
+        v_plane = sb("v_plane", [PARTS, S], U8)
+        nc.vector.tensor_copy(v_plane[:], tab_plane[:].indirect(offs_t[:]))
+        nc.gpsimd.dma_start(out=moved_plane[0:100, :].bitcast(I32), in_=v_plane[4:104, :].bitcast(I32))
+        planes = [v_plane, moved_plane]
+        place_slice(0, left0)
+        ident = sb("ident", [PARTS, PARTS], F32, "w3_woven0")
+        make_identity(nc, ident[:])
+        base_rows = sb("base_rows", [PARTS, PARTS], F32, "w3_raw0")
+        nc.gpsimd.memset(base_rows[:], 0.0)
+        nc.sync.dma_start(out=base_rows[0:SLICES, :], in_=base.rearrange("(c p) -> c p", p=PARTS))
+        tab_t = [sb("tab_t%d" % a, [PARTS, T], U32) for a in range(2)]
+        for a in range(2):
+            nc.sync.dma_start(out=tab_t[a][:].bitcast(I32), in_=tab_words[a].rearrange("p t i -> p (t i)").bitcast(I32))
+        w1_t = sb("w1_t", [PARTS, 2, 2 * H], U8)
+        nc.sync.dma_start(out=w1_t[:].bitcast(I32), in_=w1_words.rearrange("a p n -> p a n").bitcast(I32))
+        w1_plane = sb("w1_plane", [PARTS, 2, H], U8, "neg_tanh0")
+        nc.gpsimd.memset(w1_plane[:].bitcast(I32), 0)
+        load_scale_rows(nc.sync, w1_plane, w1_scales)
+        w3_woven = sb("w3_woven", [PARTS, 896, 4], BF16, "picked")
+        w3_part(1, 1, w3_raw[1], 0, w3_woven[:, 0:128, :])
+        kind_slice(1)
+        place_slice(1, left_slice(1, 3))
+        w3_part(2, 2, w3_raw[1], 128, w3_woven[:, 128:384, :])
+        w3_part(4, 2, w3_raw[2], 0, w3_woven[:, 384:640, :])
+        w3_part(6, 2, w3_raw[2], 256, w3_woven[:, 640:896, :])
+        for c in range(2, SLICES):
+            kind_slice(c)
+
+        w2_raw.append(load_rows("w2_raw2", w2, 0, 256, 256, "tab2_plane"))
+        w2_raw.append(load_rows("w2_raw3", w2, 0, 512, 512, "tab2_t"))
+        w5_plane = sb("w5_plane", [PARTS, 2, N], U8, "w3_codes4")
+        nc.gpsimd.memset(w5_plane[:].bitcast(I32), 0)
+        load_scale_rows(nc.sync, w5_plane, w5_scales)
+        w5_t = sb("w5_t", [PARTS, 2, N], U32, "w3_codes6")
+        nc.sync.dma_start(out=w5_t[:].bitcast(I32), in_=w5_words.rearrange("a p c i -> p a (c i)").bitcast(I32))
+
+        base_bank = bank(7, "base_bank")
+        nc.tensor.transpose(base_bank[:, 0:PARTS], base_rows[:], ident[:])
+        base_cols = sb("base_cols", [PARTS, SLICES], F32)
+        nc.scalar.copy(base_cols[:], base_bank[:, 0:SLICES])
+        nc.scalar.activation(warm_out[:, 1:2], neg_tanh[7][:, 0:1], ACT.Sqrt, bias=base_cols[:, 0:1], scale=0.0)
+
+        picked = sb("picked", [PARTS, 2 * S], U32)
+        v = {}
+        for a in range(2):
+            for h in range(2):
+                v[a, h] = picked[:, S * h + HALF * a : S * h + HALF * a + HALF]
+                nc.vector.tensor_copy(v[a, h], tab_t[a][:].indirect(offs_t[:, 32 * h : 32 * h + 32]))
+
+        place_slice(2, left_slice(2, 7))
+        zt = {}
+        z_codes = {}
+
+        def root_slice(c):
+            roots = []
+            for h in range(2):
+                acc = bank(h if c < 7 else (7, 4)[h], "intake%d_%d" % (c, h))
+                for a in range(2):
+                    mx(
+                        acc[:],
+                        w1_t[:, a, 256 * c : 256 * c + 256].bitcast(FP4X4),
+                        w1_plane[:, a, 128 * c : 128 * c + 128],
+                        v[a, h].bitcast(FP8X4),
+                        planes[a][:, HALF * h : HALF * h + HALF],
+                        a == 0,
+                        a == 1,
+                    )
+                size = sb("size%d_%d" % (c, h), [PARTS, HALF], F32, "size%d" % h)
+                nc.scalar.activation(size[:], acc[:], ACT.Abs)
+                root = sb("root%d_%d" % (c, h), [PARTS, HALF], F32, "root%d" % ((2 * c + h) % 4))
+                nc.scalar.activation(root[:], size[:], ACT.Sqrt, bias=base_cols[:, c : c + 1])
+                roots.append(root)
+            return roots
+
+        def difference(c, h, root, index):
+            b, cc = divmod(c, 4)
+            acc = bank(index, "diff%d_%d" % (c, h))
+            for jt in range(4):
+                nc.tensor.matmul(
+                    acc[:, 128 * jt : 128 * jt + 128], root[:, 128 * jt : 128 * jt + 128], ident[:],
+                    start=(jt == 0), stop=False, is_transpose=True,
+                )
+            for jt in range(4):
+                col = HALF * h + 128 * jt
+                nc.tensor.matmul(
+                    acc[:, 128 * jt : 128 * jt + 128], pages[c % PAGES][:, col : col + 128], ident[:],
+                    start=False, stop=(jt == 3), is_transpose=True,
+                )
+            if cc == 0:
+                zt[b, h] = sb("zt%d_%d" % (b, h), [PARTS, 4, 2, PARTS, 2], BF16)
+            nc.scalar.copy(
+                zt[b, h][:, :, :, 32 * cc : 32 * cc + 32, :],
+                acc[:].rearrange("j (jt q u e) -> j jt u q e", jt=4, u=2, e=2),
+            )
+
+        def turn_back(b, h, copy):
+            words = zt[b, h][:].rearrange("j jt u p e -> j (jt u p e)").bitcast(F32)
+            woven = sb("z_woven%d_%d" % (b, h), [PARTS, HALF, 4], BF16)
+            woven_words = woven[:].rearrange("p j t -> p (j t)").bitcast(F32)
+            for s in range(2):
+                acc = bank(4 + s, "back%d_%d_%d" % (b, h, s))
+                for i in range(4):
+                    col = 512 * s + 128 * i
+                    nc.tensor.transpose(acc[:, 128 * i : 128 * i + 128], words[:, col : col + 128], ident[:])
+                copy(
+                    woven_words[:, 512 * s : 512 * s + 512].rearrange("p (jt j u) -> p jt j u", jt=2, u=2),
+                    acc[:].rearrange("p (jt u j) -> p jt j u", jt=2, u=2),
+                )
+            z_codes[b, h] = quantize("z%d_%d" % (b, h), woven[:], HALF)
+
+        for c in range(SLICES):
+            roots = root_slice(c)
+            for h in range(2):
+                difference(c, h, roots[h], (3, 6)[c % 2] if h else 2)
+            if c == 3:
+                turn_back(0, 0, nc.scalar.copy)
+                turn_back(0, 1, nc.vector.tensor_copy)
+            if c + 3 < SLICES:
+                place_slice(c + 3, left_slice(c + 3, 5 if c == 3 else (3, 6)[c % 2]))
+            if c == 0:
+                w4_raw = [load_rows("w4_raw0", w4, 0, 0, N, "tab2_plane")]
+            if c == 4:
+                w4_raw.append(load_rows("w4_raw1", w4, 512, 0, N, "tab2_t"))
+
+        w4_q = []
+        w4_woven = sb("w4_woven", [PARTS, 2, N, 4], BF16, "neg_b1")
+        for b in range(2):
+            nc.vector.tensor_copy(
+                w4_woven[:, b, :, :].rearrange("p (c i) t -> p c t i", i=4),
+                w4_raw[b][:].rearrange("p t (c i) -> p c t i", i=4),
+            )
+            w4_q.append(quantize("w4_%d" % b, w4_woven[:, b, :, :], N))
+        turn_back(1, 0, nc.scalar.copy)
+        turn_back(1, 1, nc.scalar.copy)
+
+        bank_pairs = [(2, 0), (6, 1), (2, 7), (6, 3), (4, 0), (5, 1), (2, 7), (6, 3)]
+        for h in range(2):
+            for n in range(4):
+                cols = slice(128 * n, 128 * n + 128)
+                i1, i2 = bank_pairs[4 * h + n]
+                y2 = bank(i2, "y2_%d_%d" % (h, n))
+                y1 = bank(i1, "y1_%d_%d" % (h, n))
+                for b in range(2):
+                    zc, zp = z_codes[b, h]
+                    mx(y2[:], w5_t[:, b, cols].bitcast(FP8X4), w5_plane[:, b, cols], zc[:].bitcast(FP8X4), zp[:], b == 0, b == 1)
+                for b in range(2):
+                    zc, zp = z_codes[b, h]
+                    wc, wp = w4_q[b]
+                    mx(y1[:], wc[:, cols].bitcast(FP8X4), wp[:, cols], zc[:].bitcast(FP8X4), zp[:], b == 0, b == 1)
+                held = sb("held%d_%d" % (h, n), [PARTS, HALF], F32, "size%d" % (n % 2))
+                nc.scalar.copy(held[:], y2[:])
+                low = sb("low%d_%d" % (h, n), [PARTS, HALF], F32, "root%d" % n)
+                nc.vector.tensor_tensor(low[:], y1[:], held[:], ALU.min)
+                nc.sync.dma_start(out=out[cols, HALF * h : HALF * h + HALF], in_=low[:])

@@ -18,9 +18,20 @@ ACT = mybir.ActivationFunctionType
 ALU = mybir.AluOpType
 
 PARTS = 128
+PASS = 512
 HALF = 512
 SLICES = H // PARTS
-PAGES = 3
+AHEAD = 3
+PAGES = AHEAD
+
+INTAKE_BANKS = (0, 1)
+DIFF_BANK = 2
+DIFF_LEFT_BANKS = (3, 6)
+BACK_BANKS = (4, 5)
+SPARE_BANK = 7
+KIND_BANKS = (6, 7, 6, 7, 0, 1, 1, 0)
+LAST_INTAKE_BANKS = (SPARE_BANK, BACK_BANKS[0])
+SCORE_BANKS = ((2, 0), (6, 1), (2, 7), (6, 3), (4, 0), (5, 1), (2, 7), (6, 3))
 
 
 def tile_list_ration_adequacy_scores_kernel(
@@ -38,27 +49,34 @@ def tile_list_ration_adequacy_scores_kernel(
         def bank(index, name):
             return psum.tile([PARTS, HALF], F32, name=name, tag="bank%d" % index)
 
-        def load_scale_rows(queue, plane, scales):
+        def block(i, width=PARTS):
+            return slice(width * i, width * (i + 1))
+
+        def load_planes(plane, scales):
             for q in range(4):
-                queue.dma_start(
+                nc.sync.dma_start(
                     out=plane[32 * q : 32 * q + 4, :, :].bitcast(I32),
                     in_=scales[:, 4 * q : 4 * q + 4, :].rearrange("a r n -> r a n").bitcast(I32),
                 )
 
+        def load_words(tile, words):
+            nc.sync.dma_start(out=tile[:].bitcast(I32), in_=words.rearrange("p t i -> p (t i)").bitcast(I32))
+
         def load_rows(name, w, row0, col0, cols, tag=None):
             raw = sb(name, [PARTS, 4, cols], F32, tag)
             nc.sync.dma_start(
-                out=raw[:], in_=w[row0 : row0 + 512, col0 : col0 + cols].rearrange("(p t) c -> p t c", t=4)
+                out=raw[:], in_=w[row0 : row0 + PASS, col0 : col0 + cols].rearrange("(p t) c -> p t c", t=4)
             )
             return raw
 
-        def weave(copy, name, raw, col0, cols, tag=None):
-            woven = sb(name, [PARTS, cols, 4], BF16, tag)
+        def weave(copy, woven, raw):
             copy(
-                woven[:].rearrange("p (c i) t -> p c t i", i=4),
-                raw[:, :, col0 : col0 + cols].rearrange("p t (c i) -> p c t i", i=4),
+                woven.rearrange("p (c i) t -> p c t i", i=4),
+                raw.rearrange("p t (c i) -> p c t i", i=4),
             )
-            return woven
+
+        def scalar_cast(woven, raw):
+            nc.scalar.activation(woven, raw, ACT.Copy)
 
         def quantize(name, woven, cols, tag=None, plane_tag=None):
             codes = sb(name + "_codes", [PARTS, cols], U32, tag)
@@ -74,15 +92,16 @@ def tile_list_ration_adequacy_scores_kernel(
             )
 
         tab2_plane = sb("tab2_plane", [PARTS, TB], U8)
-        warm = sb("warm", [PARTS, 1], F32)
-        nc.vector.memset(warm[:], 0.0)
-        warm_out = sb("warm_out", [PARTS, 2], F32)
-        nc.scalar.activation(warm_out[:, 0:1], warm[:], ACT.Tanh)
+        nc.gpsimd.memset(tab2_plane[:].bitcast(I32), 0)
+        for q in range(4):
+            nc.gpsimd.dma_start(
+                out=tab2_plane[32 * q : 32 * q + 4, :].bitcast(I32),
+                in_=tab2_scales[0, 4 * q : 4 * q + 4, :].bitcast(I32),
+            )
         tab_plane = sb("tab_plane", [PARTS, T], U8)
-        nc.vector.memset(tab_plane[:].bitcast(I32), 0)
         moved_plane = sb("moved_plane", [PARTS, S], U8)
         pages = [sb("page%d" % i, [PARTS, S], F32) for i in range(PAGES)]
-        for words in [pages[0][:], moved_plane[:].bitcast(I32), pages[1][:], pages[2][:]]:
+        for words in [tab_plane[:].bitcast(I32), pages[0][:], moved_plane[:].bitcast(I32), pages[1][:], pages[2][:]]:
             last = words.shape[1] - 1
             nc.vector.memset(words[:, 0:last], 0)
             nc.vector.memset(words[:, last : last + 1], 0)
@@ -94,15 +113,10 @@ def tile_list_ration_adequacy_scores_kernel(
 
         offs2_t = sb("offs2_t", [PARTS, P // 16], U16)
         nc.sync.dma_start(offs2_t[:], offs2)
-        for q in range(4):
-            nc.sync.dma_start(
-                out=tab2_plane[32 * q : 32 * q + 32, :].bitcast(I32),
-                in_=tab2_scales[0, 4 * q : 4 * q + 4, :].bitcast(I32).unsqueeze(0).to_broadcast([8, 4, TB // 4]),
-            )
         tab2_t = sb("tab2_t", [PARTS, TB], U32)
-        nc.sync.dma_start(out=tab2_t[:].bitcast(I32), in_=tab2_words[0].rearrange("p t i -> p (t i)").bitcast(I32))
-        w3_raw = [load_rows("w3_raw0", w3, 0, 0, 128)]
-        w2_raw = [load_rows("w2_raw0", w2, 0, 0, 256)]
+        load_words(tab2_t, tab2_words[0])
+        w3_raw = [load_rows("w3_raw0", w3, 0, 0, PARTS)]
+        w2_raw = [load_rows("w2_raw0", w2, 0, 0, 2 * PARTS)]
         offs_t = sb("offs_t", [PARTS, S // 16], U16)
         nc.sync.dma_start(offs_t[:], offs)
         wgs_t = sb("wgs_t", [PARTS, P], F32)
@@ -110,61 +124,57 @@ def tile_list_ration_adequacy_scores_kernel(
         pos_t = sb("pos_t", [PARTS, P // 16], U16)
         nc.sync.dma_start(pos_t[:], pos1)
 
-        def w2_piece(c):
-            if c < 2:
-                return w2_raw[0], 128 * c
-            if c < 4:
-                return w2_raw[1], 128 * (c - 2)
-            return w2_raw[2], 128 * (c - 4)
-
-        v2_plane = sb("v2_plane", [PARTS, P], U8)
-        nc.vector.tensor_copy(v2_plane[:], tab2_plane[:].indirect(offs2_t[:]))
         v2 = sb("v2", [PARTS, P], U32)
         nc.vector.tensor_copy(v2[:], tab2_t[:].indirect(offs2_t[:]))
+        v2_plane = sb("v2_plane", [PARTS, P], U8)
+        nc.vector.tensor_copy(v2_plane[:], tab2_plane[:].indirect(offs2_t[:]))
 
-        w3_raw.append(load_rows("w3_raw1", w3, 0, 128, 384, "tab2_plane"))
-        w3_raw.append(load_rows("w3_raw2", w3, 0, 512, 512, "tab2_t"))
-        neg_tanh = {}
+        w3_raw.append(load_rows("w3_raw1", w3, 0, PARTS, 3 * PARTS, "tab2_t"))
+        w3_raw.append(load_rows("w3_raw2", w3, 0, 4 * PARTS, 4 * PARTS, "tab2_plane"))
 
         w3_q = {}
+        neg_tanh = {}
 
-        def w3_part(first, count, raw, col0, woven):
-            nc.scalar.copy(
-                woven.rearrange("p (c i) t -> p c t i", i=4),
-                raw[:, :, col0 : col0 + 128 * count].rearrange("p t (c i) -> p c t i", i=4),
-            )
-            codes, plane = quantize("w3_%d" % first, woven, 128 * count, "w3_codes%d" % first if first else "picked", None if first else "tab_t0")
+        def w3_part(copy, first, count, raw, woven, tag, plane_tag=None):
+            weave(copy, woven, raw)
+            codes, plane = quantize("w3_%d" % first, woven, PARTS * count, tag, plane_tag)
             for i in range(count):
-                w3_q[first + i] = (codes[:, 128 * i : 128 * i + 128], plane[:, 128 * i : 128 * i + 128])
+                w3_q[first + i] = (codes[:, block(i)], plane[:, block(i)])
 
         def kind_slice(c):
             codes, plane = w3_q[c]
-            acc = bank((6, 7, 6, 7, 0, 1, 1, 0)[c], "kind%d" % c)
+            acc = bank(KIND_BANKS[c], "kind%d" % c)
             mx(acc[:], codes.bitcast(FP8X4), plane, v2[:].bitcast(FP8X4), v2_plane[:], True, True)
             neg_tanh[c] = sb("neg_tanh%d" % c, [PARTS, P], F32)
             nc.scalar.activation(neg_tanh[c][:], acc[:], ACT.Tanh, scale=-1.0)
 
-        def left_slice(c, index):
-            raw, col0 = w2_piece(c)
-            copy = nc.scalar.copy if c == 0 else nc.vector.tensor_copy
-            codes, plane = quantize("w2_%d" % c, weave(copy, "w2_woven%d" % c, raw, col0, 128, ("v_plane", "tab_plane", "tab_t1")[min(c, 2)])[:], 128, "w2_codes%d" % (c % 2) if c else "w1_t", None if c else "tab_t1")
+        def left_slice(c, index, copy, raw, woven_tag, tag, plane_tag=None):
+            woven = sb("w2_woven%d" % c, [PARTS, PARTS, 4], BF16, woven_tag)
+            weave(copy, woven[:], raw)
+            codes, plane = quantize("w2_%d" % c, woven[:], PARTS, tag, plane_tag)
             acc = bank(index, "left%d" % c)
             mx(acc[:], codes[:].bitcast(FP8X4), plane[:], v2[:].bitcast(FP8X4), v2_plane[:], True, True)
             return acc
 
-        def place_slice(c, acc):
-            neg_b = sb("neg_b%d" % c, [PARTS, P], F32, "neg_b%d" % (c % 2) if c else "tab_plane")
-            nc.vector.tensor_tensor(neg_b[:], acc[:], neg_tanh[c][:], ALU.mult)
+        def later_left_slice(c, index):
+            raw = w2_raw[1][:, :, block(c - 2)] if c < 4 else w2_raw[2][:, :, block(c - 4)]
+            return left_slice(c, index, nc.vector.tensor_copy, raw, "tab_t1", "w2_codes%d" % (c % 2))
+
+        def place_slice(c, left, tag):
+            neg_b = sb("neg_b%d" % c, [PARTS, P], F32, tag)
+            nc.vector.tensor_tensor(neg_b[:], left[:], neg_tanh[c][:], ALU.mult)
             nc.vector.tensor_tensor(pages[c % PAGES][:].indirect(pos_t[:]), neg_b[:], wgs_t[:], ALU.mult)
 
-        w3_part(0, 1, w3_raw[0], 0, sb("w3_woven0", [PARTS, 128, 4], BF16)[:])
+        w3_woven0 = sb("w3_woven0", [PARTS, PARTS, 4], BF16)
+        w3_part(scalar_cast, 0, 1, w3_raw[0][:], w3_woven0[:], "picked", "tab_t0")
         kind_slice(0)
-        left0 = left_slice(0, 2)
+        left0 = left_slice(0, DIFF_BANK, nc.scalar.copy, w2_raw[0][:, :, block(0)], "v_plane", "w1_t", "tab_t1")
         v_plane = sb("v_plane", [PARTS, S], U8)
         nc.vector.tensor_copy(v_plane[:], tab_plane[:].indirect(offs_t[:]))
         nc.gpsimd.dma_start(out=moved_plane[0:100, :].bitcast(I32), in_=v_plane[4:104, :].bitcast(I32))
-        planes = [v_plane, moved_plane]
-        place_slice(0, left0)
+        v_planes = [v_plane, moved_plane]
+        place_slice(0, left0, "tab_plane")
+
         ident = sb("ident", [PARTS, PARTS], F32, "w3_woven0")
         make_identity(nc, ident[:])
         base_rows = sb("base_rows", [PARTS, PARTS], F32, "w3_raw0")
@@ -172,145 +182,151 @@ def tile_list_ration_adequacy_scores_kernel(
         nc.sync.dma_start(out=base_rows[0:SLICES, :], in_=base.rearrange("(c p) -> c p", p=PARTS))
         tab_t = [sb("tab_t%d" % a, [PARTS, T], U32) for a in range(2)]
         for a in range(2):
-            nc.sync.dma_start(out=tab_t[a][:].bitcast(I32), in_=tab_words[a].rearrange("p t i -> p (t i)").bitcast(I32))
+            load_words(tab_t[a], tab_words[a])
         w1_t = sb("w1_t", [PARTS, 2, 2 * H], U8)
         nc.sync.dma_start(out=w1_t[:].bitcast(I32), in_=w1_words.rearrange("a p n -> p a n").bitcast(I32))
         w1_plane = sb("w1_plane", [PARTS, 2, H], U8, "neg_tanh0")
         nc.gpsimd.memset(w1_plane[:].bitcast(I32), 0)
-        load_scale_rows(nc.sync, w1_plane, w1_scales)
-        w3_woven = sb("w3_woven", [PARTS, 896, 4], BF16, "picked")
-        w3_part(1, 1, w3_raw[1], 0, w3_woven[:, 0:128, :])
+        load_planes(w1_plane, w1_scales)
+
+        w3_woven = sb("w3_woven", [PARTS, H - PARTS, 4], BF16, "picked")
+        w3_part(nc.scalar.copy, 1, 1, w3_raw[1][:, :, block(0)], w3_woven[:, block(0), :], "w3_codes1")
         kind_slice(1)
-        place_slice(1, left_slice(1, 3))
-        w3_part(2, 2, w3_raw[1], 128, w3_woven[:, 128:384, :])
-        w3_part(4, 2, w3_raw[2], 0, w3_woven[:, 384:640, :])
-        w3_part(6, 2, w3_raw[2], 256, w3_woven[:, 640:896, :])
+        left1 = left_slice(
+            1, DIFF_LEFT_BANKS[0], nc.vector.tensor_copy, w2_raw[0][:, :, block(1)], "tab_plane", "w2_codes1"
+        )
+        place_slice(1, left1, "neg_b1")
+        for first, raw, col0 in ((2, w3_raw[1], PARTS), (4, w3_raw[2], 0), (6, w3_raw[2], 2 * PARTS)):
+            woven = w3_woven[:, PARTS * (first - 1) : PARTS * (first + 1), :]
+            w3_part(nc.scalar.copy, first, 2, raw[:, :, col0 : col0 + 2 * PARTS], woven, "w3_codes%d" % first)
         for c in range(2, SLICES):
             kind_slice(c)
 
-        w2_raw.append(load_rows("w2_raw2", w2, 0, 256, 256, "tab2_plane"))
-        w2_raw.append(load_rows("w2_raw3", w2, 0, 512, 512, "tab2_t"))
+        w2_raw.append(load_rows("w2_raw1", w2, 0, 2 * PARTS, 2 * PARTS, "tab2_t"))
+        w2_raw.append(load_rows("w2_raw2", w2, 0, 4 * PARTS, 4 * PARTS, "tab2_plane"))
         w5_plane = sb("w5_plane", [PARTS, 2, N], U8, "w3_codes4")
         nc.gpsimd.memset(w5_plane[:].bitcast(I32), 0)
-        load_scale_rows(nc.sync, w5_plane, w5_scales)
+        load_planes(w5_plane, w5_scales)
         w5_t = sb("w5_t", [PARTS, 2, N], U32, "w3_codes6")
         nc.sync.dma_start(out=w5_t[:].bitcast(I32), in_=w5_words.rearrange("a p c i -> p a (c i)").bitcast(I32))
 
-        base_bank = bank(7, "base_bank")
+        base_bank = bank(SPARE_BANK, "base_bank")
         nc.tensor.transpose(base_bank[:, 0:PARTS], base_rows[:], ident[:])
         base_cols = sb("base_cols", [PARTS, SLICES], F32)
         nc.scalar.copy(base_cols[:], base_bank[:, 0:SLICES])
-        nc.scalar.activation(warm_out[:, 1:2], neg_tanh[7][:, 0:1], ACT.Sqrt, bias=base_cols[:, 0:1], scale=0.0)
 
         picked = sb("picked", [PARTS, 2 * S], U32)
         v = {}
         for a in range(2):
             for h in range(2):
-                v[a, h] = picked[:, S * h + HALF * a : S * h + HALF * a + HALF]
-                nc.vector.tensor_copy(v[a, h], tab_t[a][:].indirect(offs_t[:, 32 * h : 32 * h + 32]))
+                v[a, h] = picked[:, block(2 * h + a, HALF)]
+                nc.vector.tensor_copy(v[a, h], tab_t[a][:].indirect(offs_t[:, block(h, HALF // 16)]))
 
-        place_slice(2, left_slice(2, 7))
-        zt = {}
-        z_codes = {}
+        place_slice(2, later_left_slice(2, SPARE_BANK), "neg_b0")
+
+        turned = {}
+        z_q = {}
 
         def root_slice(c):
             roots = []
             for h in range(2):
-                acc = bank(h if c < 7 else (7, 4)[h], "intake%d_%d" % (c, h))
+                acc = bank((INTAKE_BANKS if c < SLICES - 1 else LAST_INTAKE_BANKS)[h], "intake%d_%d" % (c, h))
                 for a in range(2):
                     mx(
                         acc[:],
-                        w1_t[:, a, 256 * c : 256 * c + 256].bitcast(FP4X4),
-                        w1_plane[:, a, 128 * c : 128 * c + 128],
+                        w1_t[:, a, block(c, 2 * PARTS)].bitcast(FP4X4),
+                        w1_plane[:, a, block(c)],
                         v[a, h].bitcast(FP8X4),
-                        planes[a][:, HALF * h : HALF * h + HALF],
+                        v_planes[a][:, block(h, HALF)],
                         a == 0,
                         a == 1,
                     )
                 size = sb("size%d_%d" % (c, h), [PARTS, HALF], F32, "size%d" % h)
                 nc.scalar.activation(size[:], acc[:], ACT.Abs)
-                root = sb("root%d_%d" % (c, h), [PARTS, HALF], F32, "root%d" % ((2 * c + h) % 4))
+                root = sb("root%d_%d" % (c, h), [PARTS, HALF], F32, "root%d" % (2 * (c % 2) + h))
                 nc.scalar.activation(root[:], size[:], ACT.Sqrt, bias=base_cols[:, c : c + 1])
                 roots.append(root)
             return roots
 
         def difference(c, h, root, index):
-            b, cc = divmod(c, 4)
+            b, quarter = divmod(c, 4)
             acc = bank(index, "diff%d_%d" % (c, h))
-            for jt in range(4):
+            for g in range(4):
                 nc.tensor.matmul(
-                    acc[:, 128 * jt : 128 * jt + 128], root[:, 128 * jt : 128 * jt + 128], ident[:],
-                    start=(jt == 0), stop=False, is_transpose=True,
+                    acc[:, block(g)], root[:, block(g)], ident[:], start=(g == 0), stop=False, is_transpose=True
                 )
-            for jt in range(4):
-                col = HALF * h + 128 * jt
+            for g in range(4):
                 nc.tensor.matmul(
-                    acc[:, 128 * jt : 128 * jt + 128], pages[c % PAGES][:, col : col + 128], ident[:],
-                    start=False, stop=(jt == 3), is_transpose=True,
+                    acc[:, block(g)], pages[c % PAGES][:, block(4 * h + g)], ident[:],
+                    start=False, stop=(g == 3), is_transpose=True,
                 )
-            if cc == 0:
-                zt[b, h] = sb("zt%d_%d" % (b, h), [PARTS, 4, 2, PARTS, 2], BF16)
+            if quarter == 0:
+                turned[b, h] = sb("turned%d_%d" % (b, h), [PARTS, 4, 2, PARTS, 2], BF16)
             nc.scalar.copy(
-                zt[b, h][:, :, :, 32 * cc : 32 * cc + 32, :],
-                acc[:].rearrange("j (jt q u e) -> j jt u q e", jt=4, u=2, e=2),
+                turned[b, h][:, :, :, block(quarter, 32), :],
+                acc[:].rearrange("j (g q u e) -> j g u q e", g=4, u=2, e=2),
             )
 
         def turn_back(b, h, copy):
-            words = zt[b, h][:].rearrange("j jt u p e -> j (jt u p e)").bitcast(F32)
+            words = turned[b, h][:].rearrange("j g u p e -> j (g u p e)").bitcast(F32)
             woven = sb("z_woven%d_%d" % (b, h), [PARTS, HALF, 4], BF16)
             woven_words = woven[:].rearrange("p j t -> p (j t)").bitcast(F32)
             for s in range(2):
-                acc = bank(4 + s, "back%d_%d_%d" % (b, h, s))
+                acc = bank(BACK_BANKS[s], "back%d_%d_%d" % (b, h, s))
                 for i in range(4):
-                    col = 512 * s + 128 * i
-                    nc.tensor.transpose(acc[:, 128 * i : 128 * i + 128], words[:, col : col + 128], ident[:])
+                    nc.tensor.transpose(acc[:, block(i)], words[:, block(4 * s + i)], ident[:])
                 copy(
-                    woven_words[:, 512 * s : 512 * s + 512].rearrange("p (jt j u) -> p jt j u", jt=2, u=2),
-                    acc[:].rearrange("p (jt u j) -> p jt j u", jt=2, u=2),
+                    woven_words[:, block(s, HALF)].rearrange("p (g j u) -> p g j u", g=2, u=2),
+                    acc[:].rearrange("p (g u j) -> p g j u", g=2, u=2),
                 )
-            z_codes[b, h] = quantize("z%d_%d" % (b, h), woven[:], HALF)
+            z_q[b, h] = quantize("z%d_%d" % (b, h), woven[:], HALF)
 
+        w4_raw = []
         for c in range(SLICES):
             roots = root_slice(c)
-            for h in range(2):
-                difference(c, h, roots[h], (3, 6)[c % 2] if h else 2)
-            if c == 3:
+            difference(c, 0, roots[0], DIFF_BANK)
+            difference(c, 1, roots[1], DIFF_LEFT_BANKS[c % 2])
+            first_pass_done = c == 3
+            if first_pass_done:
                 turn_back(0, 0, nc.scalar.copy)
                 turn_back(0, 1, nc.vector.tensor_copy)
-            if c + 3 < SLICES:
-                place_slice(c + 3, left_slice(c + 3, 5 if c == 3 else (3, 6)[c % 2]))
-            if c == 0:
-                w4_raw = [load_rows("w4_raw0", w4, 0, 0, N, "tab2_plane")]
-            if c == 4:
-                w4_raw.append(load_rows("w4_raw1", w4, 512, 0, N, "tab2_t"))
+            later = c + AHEAD
+            if later < SLICES:
+                index = BACK_BANKS[1] if first_pass_done else DIFF_LEFT_BANKS[c % 2]
+                place_slice(later, later_left_slice(later, index), "neg_b%d" % (later % 2))
+            if later == 3:
+                w4_raw.append(load_rows("w4_raw0", w4, 0, 0, N, "tab2_t"))
+            if later == SLICES - 1:
+                w4_raw.append(load_rows("w4_raw1", w4, PASS, 0, N, "tab2_plane"))
 
         w4_q = []
         w4_woven = sb("w4_woven", [PARTS, 2, N, 4], BF16, "neg_b1")
         for b in range(2):
-            nc.vector.tensor_copy(
-                w4_woven[:, b, :, :].rearrange("p (c i) t -> p c t i", i=4),
-                w4_raw[b][:].rearrange("p t (c i) -> p c t i", i=4),
-            )
+            weave(nc.vector.tensor_copy, w4_woven[:, b, :, :], w4_raw[b][:])
             w4_q.append(quantize("w4_%d" % b, w4_woven[:, b, :, :], N))
         turn_back(1, 0, nc.scalar.copy)
         turn_back(1, 1, nc.scalar.copy)
 
-        bank_pairs = [(2, 0), (6, 1), (2, 7), (6, 3), (4, 0), (5, 1), (2, 7), (6, 3)]
         for h in range(2):
-            for n in range(4):
-                cols = slice(128 * n, 128 * n + 128)
-                i1, i2 = bank_pairs[4 * h + n]
-                y2 = bank(i2, "y2_%d_%d" % (h, n))
-                y1 = bank(i1, "y1_%d_%d" % (h, n))
+            for n in range(N // PARTS):
+                index1, index2 = SCORE_BANKS[4 * h + n]
+                y2 = bank(index2, "y2_%d_%d" % (h, n))
+                y1 = bank(index1, "y1_%d_%d" % (h, n))
                 for b in range(2):
-                    zc, zp = z_codes[b, h]
-                    mx(y2[:], w5_t[:, b, cols].bitcast(FP8X4), w5_plane[:, b, cols], zc[:].bitcast(FP8X4), zp[:], b == 0, b == 1)
+                    z_codes, z_plane = z_q[b, h]
+                    mx(
+                        y2[:], w5_t[:, b, block(n)].bitcast(FP8X4), w5_plane[:, b, block(n)],
+                        z_codes[:].bitcast(FP8X4), z_plane[:], b == 0, b == 1,
+                    )
                 for b in range(2):
-                    zc, zp = z_codes[b, h]
-                    wc, wp = w4_q[b]
-                    mx(y1[:], wc[:, cols].bitcast(FP8X4), wp[:, cols], zc[:].bitcast(FP8X4), zp[:], b == 0, b == 1)
+                    z_codes, z_plane = z_q[b, h]
+                    w4_codes, w4_plane = w4_q[b]
+                    mx(
+                        y1[:], w4_codes[:, block(n)].bitcast(FP8X4), w4_plane[:, block(n)],
+                        z_codes[:].bitcast(FP8X4), z_plane[:], b == 0, b == 1,
+                    )
                 held = sb("held%d_%d" % (h, n), [PARTS, HALF], F32, "size%d" % (n % 2))
                 nc.scalar.copy(held[:], y2[:])
                 low = sb("low%d_%d" % (h, n), [PARTS, HALF], F32, "root%d" % n)
                 nc.vector.tensor_tensor(low[:], y1[:], held[:], ALU.min)
-                nc.sync.dma_start(out=out[cols, HALF * h : HALF * h + HALF], in_=low[:])
+                nc.sync.dma_start(out=out[block(n), block(h, HALF)], in_=low[:])

from contextlib import ExitStack

import concourse.mybir as mybir
from concourse.masks import make_identity

K, K2, H, N, T, TB, S, P = 1024, 512, 1024, 512, 4096, 2048, 1024, 512
FLOPS = 2 * K * H * S + 2 * 2 * K2 * H * P + 2 * 2 * H * N * S

F32 = mybir.dt.float32
BF16 = mybir.dt.bfloat16
I32 = mybir.dt.int32
U32 = mybir.dt.uint32
U16 = mybir.dt.uint16
U8 = mybir.dt.uint8
FP8X4 = mybir.dt.float8_e4m3fn_x4
FP4X4 = mybir.dt.float4_e2m1fn_x4
ACT = mybir.ActivationFunctionType
ALU = mybir.AluOpType

PARTS = 128
PASS = 512
HALF = 512
SLICES = H // PARTS
AHEAD = 3
PAGES = AHEAD

INTAKE_BANKS = (0, 1)
DIFF_BANK = 2
DIFF_LEFT_BANKS = (3, 6)
BACK_BANKS = (4, 5)
SPARE_BANK = 7
KIND_BANKS = (6, 7, 6, 7, 0, 1, 1, 0)
LAST_INTAKE_BANKS = (SPARE_BANK, BACK_BANKS[0])
SCORE_BANKS = ((2, 0), (6, 1), (2, 7), (6, 3), (4, 0), (5, 1), (2, 7), (6, 3))


def tile_list_ration_adequacy_scores_kernel(
    tc, tab_words, tab_scales, offs, tab2_words, tab2_scales, offs2, pos1, w1_words, w1_scales,
    base, w2, w3, wgs, w4, w5_words, w5_scales, out,
):
    nc = tc.nc
    with ExitStack() as ctx:
        keep = ctx.enter_context(tc.tile_pool(name="keep", bufs=1))
        psum = ctx.enter_context(tc.psum_pool(name="psum", bufs=1))

        def sb(name, shape, dtype, tag=None):
            return keep.tile(shape, dtype, name=name, tag=tag or name, align_bytes=64)

        def bank(index, name):
            return psum.tile([PARTS, HALF], F32, name=name, tag="bank%d" % index)

        def block(i, width=PARTS):
            return slice(width * i, width * (i + 1))

        def load_planes(plane, scales):
            for q in range(4):
                nc.sync.dma_start(
                    out=plane[32 * q : 32 * q + 4, :, :].bitcast(I32),
                    in_=scales[:, 4 * q : 4 * q + 4, :].rearrange("a r n -> r a n").bitcast(I32),
                )

        def load_words(tile, words):
            nc.sync.dma_start(out=tile[:].bitcast(I32), in_=words.rearrange("p t i -> p (t i)").bitcast(I32))

        def load_rows(name, w, row0, col0, cols, tag=None):
            raw = sb(name, [PARTS, 4, cols], F32, tag)
            nc.sync.dma_start(
                out=raw[:], in_=w[row0 : row0 + PASS, col0 : col0 + cols].rearrange("(p t) c -> p t c", t=4)
            )
            return raw

        def weave(copy, woven, raw):
            copy(
                woven.rearrange("p (c i) t -> p c t i", i=4),
                raw.rearrange("p t (c i) -> p c t i", i=4),
            )

        def scalar_cast(woven, raw):
            nc.scalar.activation(woven, raw, ACT.Copy)

        def quantize(name, woven, cols, tag=None, plane_tag=None):
            codes = sb(name + "_codes", [PARTS, cols], U32, tag)
            plane = sb(name + "_plane", [PARTS, cols], U8, plane_tag)
            nc.vector.quantize_mx(
                out=codes[:].bitcast(FP8X4), scales=plane[:], in_=woven.rearrange("p c t -> p (c t)")
            )
            return codes, plane

        def mx(acc, lhs, lhs_plane, rhs, rhs_plane, start, stop):
            nc.tensor.matmul_mx(
                out=acc, lhsT=lhs, lhsT_scale=lhs_plane, rhs=rhs, rhs_scale=rhs_plane, start=start, stop=stop
            )

        tab2_plane = sb("tab2_plane", [PARTS, TB], U8)
        nc.gpsimd.memset(tab2_plane[:].bitcast(I32), 0)
        for q in range(4):
            nc.gpsimd.dma_start(
                out=tab2_plane[32 * q : 32 * q + 4, :].bitcast(I32),
                in_=tab2_scales[0, 4 * q : 4 * q + 4, :].bitcast(I32),
            )
        tab_plane = sb("tab_plane", [PARTS, T], U8)
        moved_plane = sb("moved_plane", [PARTS, S], U8)
        pages = [sb("page%d" % i, [PARTS, S], F32) for i in range(PAGES)]
        for words in [tab_plane[:].bitcast(I32), pages[0][:], moved_plane[:].bitcast(I32), pages[1][:], pages[2][:]]:
            last = words.shape[1] - 1
            nc.vector.memset(words[:, 0:last], 0)
            nc.vector.memset(words[:, last : last + 1], 0)
        for q in range(4):
            nc.gpsimd.dma_start(
                out=tab_plane[32 * q : 32 * q + 8, :].bitcast(I32),
                in_=tab_scales[:, 4 * q : 4 * q + 4, :].bitcast(I32),
            )

        offs2_t = sb("offs2_t", [PARTS, P // 16], U16)
        nc.sync.dma_start(offs2_t[:], offs2)
        tab2_t = sb("tab2_t", [PARTS, TB], U32)
        load_words(tab2_t, tab2_words[0])
        w3_raw = [load_rows("w3_raw0", w3, 0, 0, PARTS)]
        w2_raw = [load_rows("w2_raw0", w2, 0, 0, 2 * PARTS)]
        offs_t = sb("offs_t", [PARTS, S // 16], U16)
        nc.sync.dma_start(offs_t[:], offs)
        wgs_t = sb("wgs_t", [PARTS, P], F32)
        nc.sync.dma_start(out=wgs_t[:], in_=wgs)
        pos_t = sb("pos_t", [PARTS, P // 16], U16)
        nc.sync.dma_start(pos_t[:], pos1)

        v2 = sb("v2", [PARTS, P], U32)
        nc.vector.tensor_copy(v2[:], tab2_t[:].indirect(offs2_t[:]))
        v2_plane = sb("v2_plane", [PARTS, P], U8)
        nc.vector.tensor_copy(v2_plane[:], tab2_plane[:].indirect(offs2_t[:]))

        w3_raw.append(load_rows("w3_raw1", w3, 0, PARTS, 3 * PARTS, "tab2_t"))
        w3_raw.append(load_rows("w3_raw2", w3, 0, 4 * PARTS, 4 * PARTS, "tab2_plane"))

        w3_q = {}
        neg_tanh = {}

        def w3_part(copy, first, count, raw, woven, tag, plane_tag=None):
            weave(copy, woven, raw)
            codes, plane = quantize("w3_%d" % first, woven, PARTS * count, tag, plane_tag)
            for i in range(count):
                w3_q[first + i] = (codes[:, block(i)], plane[:, block(i)])

        def kind_slice(c):
            codes, plane = w3_q[c]
            acc = bank(KIND_BANKS[c], "kind%d" % c)
            mx(acc[:], codes.bitcast(FP8X4), plane, v2[:].bitcast(FP8X4), v2_plane[:], True, True)
            neg_tanh[c] = sb("neg_tanh%d" % c, [PARTS, P], F32)
            nc.scalar.activation(neg_tanh[c][:], acc[:], ACT.Tanh, scale=-1.0)

        def left_slice(c, index, copy, raw, woven_tag, tag, plane_tag=None):
            woven = sb("w2_woven%d" % c, [PARTS, PARTS, 4], BF16, woven_tag)
            weave(copy, woven[:], raw)
            codes, plane = quantize("w2_%d" % c, woven[:], PARTS, tag, plane_tag)
            acc = bank(index, "left%d" % c)
            mx(acc[:], codes[:].bitcast(FP8X4), plane[:], v2[:].bitcast(FP8X4), v2_plane[:], True, True)
            return acc

        def later_left_slice(c, index):
            raw = w2_raw[1][:, :, block(c - 2)] if c < 4 else w2_raw[2][:, :, block(c - 4)]
            return left_slice(c, index, nc.vector.tensor_copy, raw, "tab_t1", "w2_codes%d" % (c % 2))

        def place_slice(c, left, tag):
            neg_b = sb("neg_b%d" % c, [PARTS, P], F32, tag)
            nc.vector.tensor_tensor(neg_b[:], left[:], neg_tanh[c][:], ALU.mult)
            nc.vector.tensor_tensor(pages[c % PAGES][:].indirect(pos_t[:]), neg_b[:], wgs_t[:], ALU.mult)

        w3_woven0 = sb("w3_woven0", [PARTS, PARTS, 4], BF16)
        w3_part(scalar_cast, 0, 1, w3_raw[0][:], w3_woven0[:], "picked", "tab_t0")
        kind_slice(0)
        left0 = left_slice(0, DIFF_BANK, nc.scalar.copy, w2_raw[0][:, :, block(0)], "v_plane", "w1_t", "tab_t1")
        v_plane = sb("v_plane", [PARTS, S], U8)
        nc.vector.tensor_copy(v_plane[:], tab_plane[:].indirect(offs_t[:]))
        nc.gpsimd.dma_start(out=moved_plane[0:100, :].bitcast(I32), in_=v_plane[4:104, :].bitcast(I32))
        v_planes = [v_plane, moved_plane]
        place_slice(0, left0, "tab_plane")

        ident = sb("ident", [PARTS, PARTS], F32, "w3_woven0")
        make_identity(nc, ident[:])
        base_rows = sb("base_rows", [PARTS, PARTS], F32, "w3_raw0")
        nc.gpsimd.memset(base_rows[:], 0.0)
        nc.sync.dma_start(out=base_rows[0:SLICES, :], in_=base.rearrange("(c p) -> c p", p=PARTS))
        tab_t = [sb("tab_t%d" % a, [PARTS, T], U32) for a in range(2)]
        for a in range(2):
            load_words(tab_t[a], tab_words[a])
        w1_t = sb("w1_t", [PARTS, 2, 2 * H], U8)
        nc.sync.dma_start(out=w1_t[:].bitcast(I32), in_=w1_words.rearrange("a p n -> p a n").bitcast(I32))
        w1_plane = sb("w1_plane", [PARTS, 2, H], U8, "neg_tanh0")
        nc.gpsimd.memset(w1_plane[:].bitcast(I32), 0)
        load_planes(w1_plane, w1_scales)

        w3_woven = sb("w3_woven", [PARTS, H - PARTS, 4], BF16, "picked")
        w3_part(nc.scalar.copy, 1, 1, w3_raw[1][:, :, block(0)], w3_woven[:, block(0), :], "w3_codes1")
        kind_slice(1)
        left1 = left_slice(
            1, DIFF_LEFT_BANKS[0], nc.vector.tensor_copy, w2_raw[0][:, :, block(1)], "tab_plane", "w2_codes1"
        )
        place_slice(1, left1, "neg_b1")
        for first, raw, col0 in ((2, w3_raw[1], PARTS), (4, w3_raw[2], 0), (6, w3_raw[2], 2 * PARTS)):
            woven = w3_woven[:, PARTS * (first - 1) : PARTS * (first + 1), :]
            w3_part(nc.scalar.copy, first, 2, raw[:, :, col0 : col0 + 2 * PARTS], woven, "w3_codes%d" % first)
        for c in range(2, SLICES):
            kind_slice(c)

        w2_raw.append(load_rows("w2_raw1", w2, 0, 2 * PARTS, 2 * PARTS, "tab2_t"))
        w2_raw.append(load_rows("w2_raw2", w2, 0, 4 * PARTS, 4 * PARTS, "tab2_plane"))
        w5_plane = sb("w5_plane", [PARTS, 2, N], U8, "w3_codes4")
        nc.gpsimd.memset(w5_plane[:].bitcast(I32), 0)
        load_planes(w5_plane, w5_scales)
        w5_t = sb("w5_t", [PARTS, 2, N], U32, "w3_codes6")
        nc.sync.dma_start(out=w5_t[:].bitcast(I32), in_=w5_words.rearrange("a p c i -> p a (c i)").bitcast(I32))

        base_bank = bank(SPARE_BANK, "base_bank")
        nc.tensor.transpose(base_bank[:, 0:PARTS], base_rows[:], ident[:])
        base_cols = sb("base_cols", [PARTS, SLICES], F32)
        nc.scalar.copy(base_cols[:], base_bank[:, 0:SLICES])

        picked = sb("picked", [PARTS, 2 * S], U32)
        v = {}
        for a in range(2):
            for h in range(2):
                v[a, h] = picked[:, block(2 * h + a, HALF)]
                nc.vector.tensor_copy(v[a, h], tab_t[a][:].indirect(offs_t[:, block(h, HALF // 16)]))

        place_slice(2, later_left_slice(2, SPARE_BANK), "neg_b0")

        turned = {}
        z_q = {}

        def root_slice(c):
            roots = []
            for h in range(2):
                acc = bank((INTAKE_BANKS if c < SLICES - 1 else LAST_INTAKE_BANKS)[h], "intake%d_%d" % (c, h))
                for a in range(2):
                    mx(
                        acc[:],
                        w1_t[:, a, block(c, 2 * PARTS)].bitcast(FP4X4),
                        w1_plane[:, a, block(c)],
                        v[a, h].bitcast(FP8X4),
                        v_planes[a][:, block(h, HALF)],
                        a == 0,
                        a == 1,
                    )
                size = sb("size%d_%d" % (c, h), [PARTS, HALF], F32, "size%d" % h)
                nc.scalar.activation(size[:], acc[:], ACT.Abs)
                root = sb("root%d_%d" % (c, h), [PARTS, HALF], F32, "root%d" % (2 * (c % 2) + h))
                nc.scalar.activation(root[:], size[:], ACT.Sqrt, bias=base_cols[:, c : c + 1])
                roots.append(root)
            return roots

        def difference(c, h, root, index):
            b, quarter = divmod(c, 4)
            acc = bank(index, "diff%d_%d" % (c, h))
            for g in range(4):
                nc.tensor.matmul(
                    acc[:, block(g)], root[:, block(g)], ident[:], start=(g == 0), stop=False, is_transpose=True
                )
            for g in range(4):
                nc.tensor.matmul(
                    acc[:, block(g)], pages[c % PAGES][:, block(4 * h + g)], ident[:],
                    start=False, stop=(g == 3), is_transpose=True,
                )
            if quarter == 0:
                turned[b, h] = sb("turned%d_%d" % (b, h), [PARTS, 4, 2, PARTS, 2], BF16)
            nc.scalar.copy(
                turned[b, h][:, :, :, block(quarter, 32), :],
                acc[:].rearrange("j (g q u e) -> j g u q e", g=4, u=2, e=2),
            )

        def turn_back(b, h, copy):
            words = turned[b, h][:].rearrange("j g u p e -> j (g u p e)").bitcast(F32)
            woven = sb("z_woven%d_%d" % (b, h), [PARTS, HALF, 4], BF16)
            woven_words = woven[:].rearrange("p j t -> p (j t)").bitcast(F32)
            for s in range(2):
                acc = bank(BACK_BANKS[s], "back%d_%d_%d" % (b, h, s))
                for i in range(4):
                    nc.tensor.transpose(acc[:, block(i)], words[:, block(4 * s + i)], ident[:])
                copy(
                    woven_words[:, block(s, HALF)].rearrange("p (g j u) -> p g j u", g=2, u=2),
                    acc[:].rearrange("p (g u j) -> p g j u", g=2, u=2),
                )
            z_q[b, h] = quantize("z%d_%d" % (b, h), woven[:], HALF)

        w4_raw = []
        for c in range(SLICES):
            roots = root_slice(c)
            difference(c, 0, roots[0], DIFF_BANK)
            difference(c, 1, roots[1], DIFF_LEFT_BANKS[c % 2])
            first_pass_done = c == 3
            if first_pass_done:
                turn_back(0, 0, nc.scalar.copy)
                turn_back(0, 1, nc.vector.tensor_copy)
            later = c + AHEAD
            if later < SLICES:
                index = BACK_BANKS[1] if first_pass_done else DIFF_LEFT_BANKS[c % 2]
                place_slice(later, later_left_slice(later, index), "neg_b%d" % (later % 2))
            if later == 3:
                w4_raw.append(load_rows("w4_raw0", w4, 0, 0, N, "tab2_t"))
            if later == SLICES - 1:
                w4_raw.append(load_rows("w4_raw1", w4, PASS, 0, N, "tab2_plane"))

        w4_q = []
        w4_woven = sb("w4_woven", [PARTS, 2, N, 4], BF16, "neg_b1")
        for b in range(2):
            weave(nc.vector.tensor_copy, w4_woven[:, b, :, :], w4_raw[b][:])
            w4_q.append(quantize("w4_%d" % b, w4_woven[:, b, :, :], N))
        turn_back(1, 0, nc.scalar.copy)
        turn_back(1, 1, nc.scalar.copy)

        for h in range(2):
            for n in range(N // PARTS):
                index1, index2 = SCORE_BANKS[4 * h + n]
                y2 = bank(index2, "y2_%d_%d" % (h, n))
                y1 = bank(index1, "y1_%d_%d" % (h, n))
                for b in range(2):
                    z_codes, z_plane = z_q[b, h]
                    mx(
                        y2[:], w5_t[:, b, block(n)].bitcast(FP8X4), w5_plane[:, b, block(n)],
                        z_codes[:].bitcast(FP8X4), z_plane[:], b == 0, b == 1,
                    )
                for b in range(2):
                    z_codes, z_plane = z_q[b, h]
                    w4_codes, w4_plane = w4_q[b]
                    mx(
                        y1[:], w4_codes[:, block(n)].bitcast(FP8X4), w4_plane[:, block(n)],
                        z_codes[:].bitcast(FP8X4), z_plane[:], b == 0, b == 1,
                    )
                held = sb("held%d_%d" % (h, n), [PARTS, HALF], F32, "size%d" % (n % 2))
                nc.scalar.copy(held[:], y2[:])
                low = sb("low%d_%d" % (h, n), [PARTS, HALF], F32, "root%d" % n)
                nc.vector.tensor_tensor(low[:], y1[:], held[:], ALU.min)
                nc.sync.dma_start(out=out[block(n), block(h, HALF)], in_=low[:])
